import numpy as np
import ml_dtypes


def mxq(x, axis, fmt="e4m3"):
    dtype, down = {"e4m3": (ml_dtypes.float8_e4m3fn, 7), "e5m2": (ml_dtypes.float8_e5m2, 14)}[fmt]
    v = np.moveaxis(np.asarray(x, np.float32).astype(ml_dtypes.bfloat16).astype(np.float64), axis, -1)
    blocks = v.reshape(v.shape[:-1] + (-1, 32))
    amax = np.abs(blocks).max(-1, keepdims=True)
    byte = np.maximum(np.where(amax > 0, np.frexp(amax)[1] - 1 + 127, 0) - down, 1)
    scale = np.exp2(byte - 127.0)
    codes = (blocks / scale).astype(np.float32).astype(dtype).astype(np.float64)
    return np.moveaxis((codes * scale).reshape(v.shape), -1, axis)


WIDE = False


def mx_kscale(k):
    if not WIDE:
        return np.ones(k)
    levels = np.array([10, -10, 5, -5, 0])
    if k % 512:
        return np.exp2(np.random.permutation(np.resize(levels, k // 32))).repeat(32)
    a = np.empty((k // 512, 16))
    for p in range(k // 512):
        a[p, :8] = np.random.permutation(np.resize(levels, 8))
        for g in range(8):
            far = levels[np.abs(levels - a[p, g]) >= 10]
            a[p, g + 8] = far[np.random.randint(len(far))]
    return np.exp2(a.ravel()).repeat(32)


def f64(x):
    return np.asarray(x).astype(np.float64)


def striped(idx):
    return np.tile(np.asarray(idx).reshape(-1, 16).T, (8, 1)).astype(np.uint16)


def unstriped(offs):
    return offs[:16].T.reshape(-1).astype(np.int64)


def rot(x):
    y = x.reshape(-1, 2, x.shape[1])
    return np.stack([-y[:, 1], y[:, 0]], axis=1).reshape(x.shape)


def bf(x):
    return np.asarray(x, np.float32).astype(ml_dtypes.bfloat16)


def planes(Y):
    r, m = Y.shape
    b = f64(bf(Y)).reshape(r // 32, 32, m)
    amax = np.abs(b).max(1)
    byte = np.clip(np.where(amax > 0, np.frexp(amax)[1] - 1 + 127 - 7, 1), 1, 254)
    codes = (b * np.exp2(127.0 - byte)[:, None, :]).reshape(r, m).astype(np.float32).astype(ml_dtypes.float8_e4m3fn).view(np.uint8)
    words = codes.reshape(r // 512, 128, 4, m).transpose(0, 1, 3, 2)
    return np.ascontiguousarray(words), np.ascontiguousarray(byte.astype(np.uint8).reshape(r // 512, 16, m))


D, T, I, Q, E, U = 512, 1024, 512, 256, 512, 1024


def setup_inputs():
    n = np.random.standard_normal
    idx = np.random.permutation(T)[:I]
    idx2 = np.random.randint(0, U, I)
    fd = mx_kscale(D)
    fi = mx_kscale(I)
    ti = np.ones(T)
    ti[idx] = fi
    return {
        "query": (n((D, Q)) * 0.4 / np.sqrt(D) * fd[:, None]).astype(np.float32),
        "keys": (n((D, T)) / fd[:, None]).astype(np.float32),
        "cosn": (np.repeat(np.round(np.cos(np.arange(D // 2)[:, None] * 0.11 + np.arange(U)[None] * 0.37) * 64) / 64, 2, axis=0)).astype(np.float32),
        "sinn": (np.repeat(np.round(np.sin(np.arange(D // 2)[:, None] * 0.11 + np.arange(U)[None] * 0.37) * 64) / 64, 2, axis=0)).astype(np.float32),
        "size": (np.random.uniform(0.5, 2.0, (1, I)) * fi).astype(np.float32),
        "vals": (n((E, T)) / ti).astype(np.float32),
        "offs": striped(idx),
        "offs2": striped(idx2),
    }


def reference(query, keys, cosn, sinn, size, vals, offs, offs2):
    idx = unstriped(offs)
    idx2 = unstriped(offs2)
    kr = rot(f64(keys)[:, idx])
    km = f64(keys)[:, idx] * f64(cosn)[:, idx2] + kr * f64(sinn)[:, idx2]
    queryq = mxq(f64(query), 0, "e4m3")
    kmq = mxq(km, 0, "e4m3")
    a = queryq.T @ kmq
    p = np.exp(a - np.max(a, axis=1, keepdims=True))
    w = p * f64(size) / np.sum(p, axis=1, keepdims=True)
    wt = w.T
    vt = f64(vals)[:, idx].T
    vtq = mxq(vt, 0, "e4m3")
    wtq = mxq(wt, 0, "e4m3")
    o = vtq.T @ wtq
    words, scales = planes(o)
    return o, words, scales

@@ -1,0 +1,193 @@
+from contextlib import ExitStack
+
+import concourse.mybir as mybir
+from concourse.masks import make_identity
+
+D, T, I, Q, E = 512, 1024, 512, 256, 512
+FLOPS = 2 * Q * I * D + 2 * E * Q * I
+BYTES = 4 * (D * Q + D * T + D * T + I + E * T + E * Q) + 2 * 2 * 128 * 32 + E * Q + 16 * Q
+
+F32 = mybir.dt.float32
+BF16 = mybir.dt.bfloat16
+I32 = mybir.dt.int32
+U32 = mybir.dt.uint32
+U16 = mybir.dt.uint16
+U8 = mybir.dt.uint8
+FP8X4 = mybir.dt.float8_e4m3fn_x4
+ALU = mybir.AluOpType
+ACT = mybir.ActivationFunctionType
+AX = mybir.AxisListType
+
+P = 128
+PACK = 4
+
+
+def tile_attend_ropeattn_pl_kernel(tc, query, keys, cosn, sinn, size, vals, offs, offs2, out_0, out_1, out_2):
+    nc = tc.nc
+    with ExitStack() as ctx:
+        sb = ctx.enter_context(tc.tile_pool(name="sb", bufs=1))
+        ps = ctx.enter_context(tc.psum_pool(name="ps", bufs=1))
+
+        tok = sb.tile([P, I // 16], U16, name="tok")
+        pos = sb.tile([P, I // 16], U16, name="pos")
+        kw = [sb.tile([P, T], F32, name="kw%d" % t) for t in range(PACK)]
+        cw = [sb.tile([P, T], F32, name="cw%d" % j) for j in range(2)]
+        sw = [sb.tile([P, T], F32, name="sw%d" % j) for j in range(2)]
+        vw = [sb.tile([P, T], F32, name="vw%d" % t) for t in range(PACK)]
+        q_raw = sb.tile([P, PACK, Q], F32, name="q_raw")
+        sz = sb.tile([P, PACK], F32, name="sz")
+        keys4 = keys.rearrange("(p t) c -> p t c", t=PACK)
+        cos4 = cosn.rearrange("(p t) c -> p t c", t=PACK)
+        sin4 = sinn.rearrange("(p t) c -> p t c", t=PACK)
+        vals4 = vals.rearrange("(p t) c -> p t c", t=PACK)
+
+        nc.sync.dma_start(tok[:], offs)
+        nc.sync.dma_start(kw[0][:], keys4[:, 0, :])
+        nc.sync.dma_start(pos[:], offs2)
+        nc.sync.dma_start(kw[1][:], keys4[:, 1, :])
+        nc.sync.dma_start(cw[0][:], cos4[:, 0, :])
+        nc.sync.dma_start(sw[0][:], sin4[:, 0, :])
+        nc.sync.dma_start(vw[0][:], vals4[:, 0, :])
+        nc.sync.dma_start(sz[:], size.rearrange("o (p j) -> p (o j)", j=PACK))
+        nc.sync.dma_start(vw[1][:], vals4[:, 1, :])
+        nc.sync.dma_start(kw[2][:], keys4[:, 2, :])
+        nc.sync.dma_start(kw[3][:], keys4[:, 3, :])
+        nc.sync.dma_start(cw[1][:], cos4[:, 2, :])
+        nc.sync.dma_start(sw[1][:], sin4[:, 2, :])
+        nc.sync.dma_start(q_raw[:], query.rearrange("(p t) c -> p t c", t=PACK))
+        nc.sync.dma_start(vw[2][:], vals4[:, 2, :])
+        nc.sync.dma_start(vw[3][:], vals4[:, 3, :])
+
+        ident = sb.tile([P, P], F32, name="ident")
+        make_identity(nc, ident[:])
+
+        warm = sb.tile([P, 8], F32, name="warm")
+        nc.vector.memset(warm[:, 0:1], 0.0)
+        nc.scalar.activation(warm[:, 4:5], warm[:, 0:1], ACT.Exp)
+
+        sz_ps = ps.tile([P, PACK, P], F32, name="sz_ps", tag="w_ps0")
+        for j in range(PACK):
+            nc.tensor.transpose(sz_ps[:, j, :], sz[:, j : j + 1].to_broadcast([P, P]), ident[:])
+        szb = sb.tile([P, P, PACK], F32, name="szb")
+        nc.scalar.copy(szb[:], sz_ps[:].rearrange("p j n -> p n j"))
+
+        kg = [sb.tile([P, I], F32, name="kg%d" % t) for t in range(PACK)]
+        cg = [sb.tile([P, I], F32, name="cg%d" % j) for j in range(2)]
+        sg = [sb.tile([P, I], F32, name="sg%d" % j) for j in range(2)]
+        pa = sb.tile([P, PACK, I], F32, name="pa")
+        pb = sb.tile([P, PACK, I], F32, name="pb")
+
+        vb = [sb.tile([P, T], BF16, name="vb%d" % r) for r in range(PACK)]
+        vg = [sb.tile([P, I], BF16, name="vg%d" % r) for r in range(PACK)]
+        vt = sb.tile([P, PACK, P, PACK], BF16, name="vt", align_bytes=64)
+        v_codes = sb.tile([P, E], U32, name="v_codes", align_bytes=64)
+        v_scales = sb.tile([P, E], U8, name="v_scales", align_bytes=64)
+
+        def rope(j):
+            t0, t1 = 2 * j, 2 * j + 1
+            nc.vector.tensor_copy(kg[t0][:], kw[t0][:].indirect(tok[:]))
+            nc.vector.tensor_copy(kg[t1][:], kw[t1][:].indirect(tok[:]))
+            nc.vector.tensor_copy(cg[j][:], cw[j][:].indirect(pos[:]))
+            nc.vector.tensor_copy(sg[j][:], sw[j][:].indirect(pos[:]))
+            nc.vector.tensor_tensor(pa[:, t0, :], kg[t0][:], cg[j][:], ALU.mult)
+            nc.vector.tensor_tensor(pa[:, t1, :], kg[t1][:], cg[j][:], ALU.mult)
+            nc.vector.tensor_tensor(pb[:, t1, :], kg[t0][:], sg[j][:], ALU.mult)
+            nc.vector.scalar_tensor_tensor(pb[:, t0, :], kg[t1][:], -1.0, sg[j][:], ALU.mult, ALU.mult)
+
+        def values(h):
+            v_ps = ps.tile([P, 2, 2, P], F32, name="v_ps%d" % h)
+            for r in (2 * h, 2 * h + 1):
+                nc.scalar.activation(vb[r][:], vw[r][:], ACT.Copy)
+                nc.scalar.activation(vg[r][:], vb[r][:].indirect(tok[:]), ACT.Copy)
+                words = vg[r][:].bitcast(F32)
+                for u in range(2):
+                    nc.tensor.transpose(v_ps[:, r - 2 * h, u, :], words[:, u::2], ident[:])
+            half = vt[:, 2 * h : 2 * h + 2, :, :].rearrange("p r m t -> p (r m t)")
+            nc.scalar.copy(half.bitcast(F32).rearrange("p (r m u) -> p r m u", r=2, u=2), v_ps[:].rearrange("p r u m -> p r m u"))
+            return half
+
+        def quantize(codes, scales, src):
+            nc.vector.quantize_mx(out=codes.bitcast(FP8X4), scales=scales, in_=src)
+
+        rope(0)
+        half0 = values(0)
+        rope(1)
+
+        qb = sb.tile([P, Q, PACK], BF16, name="qb", align_bytes=64)
+        q_codes = sb.tile([P, Q], U32, name="q_codes", align_bytes=64)
+        q_scales = sb.tile([P, Q], U8, name="q_scales", align_bytes=64)
+        nc.scalar.copy(qb[:].rearrange("p (c i) t -> p c t i", i=2), q_raw[:].rearrange("p t (c i) -> p c t i", i=2))
+
+        km = sb.tile([P, I, PACK], BF16, name="km", align_bytes=64)
+        k_codes = sb.tile([P, I], U32, name="k_codes", align_bytes=64)
+        k_scales = sb.tile([P, I], U8, name="k_scales", align_bytes=64)
+        nc.vector.tensor_tensor(
+            km[:].rearrange("p (c i) t -> p c t i", i=2),
+            pa[:].rearrange("p t (c i) -> p c t i", i=2),
+            pb[:].rearrange("p t (c i) -> p c t i", i=2),
+            ALU.add,
+        )
+        quantize(q_codes[:], q_scales[:], qb[:].rearrange("p c t -> p (c t)"))
+        quantize(k_codes[:], k_scales[:], km[:].rearrange("p c t -> p (c t)"))
+        quantize(v_codes[:, 0:256], v_scales[:, 0:256], half0)
+        half1 = values(1)
+
+        stats = [sb.tile([P, 8], F32, name="stats%d" % b) for b in range(2)]
+        sums = [sb.tile([P, 8], F32, name="sums%d" % b) for b in range(2)]
+        probs = [sb.tile([P, I], F32, name="probs%d" % b) for b in range(2)]
+        wb = [sb.tile([P, I], BF16, name="wb%d" % b) for b in range(2)]
+        wt = [sb.tile([P, P, PACK], BF16, name="wt%d" % b, align_bytes=64) for b in range(2)]
+        w_codes = [sb.tile([P, P], U32, name="w_codes%d" % b, align_bytes=64) for b in range(2)]
+        w_scales = [sb.tile([P, P], U8, name="w_scales%d" % b, align_bytes=64) for b in range(2)]
+        sc = [ps.tile([P, I], F32, name="sc%d" % b) for b in range(2)]
+        for b in range(2):
+            cols = slice(b * P, (b + 1) * P)
+            nc.tensor.matmul_mx(
+                out=sc[b][:], lhsT=q_codes[:, cols].bitcast(FP8X4), lhsT_scale=q_scales[:, cols],
+                rhs=k_codes[:].bitcast(FP8X4), rhs_scale=k_scales[:], start=True, stop=True,
+            )
+        for b in range(2):
+            nc.vector.tensor_reduce(stats[b][:, 0:1], sc[b][:], AX.X, ALU.max, negate=True)
+            nc.scalar.activation(probs[b][:], sc[b][:], ACT.Exp, bias=stats[b][:, 0:1], accum_out=sums[b][:, 0:1])
+        quantize(v_codes[:, 256:512], v_scales[:, 256:512], half1)
+        for b in range(2):
+            nc.vector.reciprocal(stats[b][:, 1:2], sums[b][:, 0:1])
+            nc.vector.scalar_tensor_tensor(
+                wb[b][:], probs[b][:], stats[b][:, 1:2], szb[:].rearrange("p n j -> p (n j)"), ALU.mult, ALU.mult
+            )
+            w_ps = ps.tile([P, 2, P], F32, name="w_ps", tag="w_ps%d" % b)
+            words = wb[b][:].bitcast(F32)
+            for u in range(2):
+                nc.tensor.transpose(w_ps[:, u, :], words[:, u::2], ident[:])
+            flat = wt[b][:].rearrange("p q t -> p (q t)")
+            nc.scalar.copy(flat.bitcast(F32).rearrange("p (q u) -> p q u", u=2), w_ps[:].rearrange("p u q -> p q u"))
+
+        o_sb = [sb.tile([P, PACK, P], F32, name="o_sb%d" % b) for b in range(2)]
+        ob = [sb.tile([P, P, PACK], BF16, name="ob%d" % b, align_bytes=64) for b in range(2)]
+        o_codes = [sb.tile([P, P], U32, name="o_codes%d" % b, align_bytes=64) for b in range(2)]
+        o_scales = sb.tile([P, Q], U8, name="o_scales", align_bytes=64)
+        out4 = out_0.rearrange("(p r) q -> p r q", r=PACK)
+        words_out = out_1[0].rearrange("l c r -> l (c r)").bitcast(I32)
+        for b in range(2):
+            cols = slice(b * P, (b + 1) * P)
+            quantize(w_codes[b][:], w_scales[b][:], wt[b][:].rearrange("p q t -> p (q t)"))
+            o_ps = ps.tile([P, PACK, P], F32, name="o_ps%d" % b)
+            for r in range(PACK):
+                rows = slice(r * P, (r + 1) * P)
+                nc.tensor.matmul_mx(
+                    out=o_ps[:, r, :], lhsT=v_codes[:, rows].bitcast(FP8X4), lhsT_scale=v_scales[:, rows],
+                    rhs=w_codes[b][:].bitcast(FP8X4), rhs_scale=w_scales[b][:], start=True, stop=True,
+                )
+            nc.scalar.copy(o_sb[b][:], o_ps[:])
+            nc.scalar.dma_start(out4[:, :, cols], o_sb[b][:])
+        for b in range(2):
+            cols = slice(b * P, (b + 1) * P)
+            nc.vector.tensor_copy(
+                ob[b][:].rearrange("p (c i) r -> p c r i", i=2), o_sb[b][:].rearrange("p r (c i) -> p c r i", i=2)
+            )
+            quantize(o_codes[b][:], o_scales[:, cols], ob[b][:].rearrange("p q r -> p (q r)"))
+            nc.sync.dma_start(words_out[:, cols], o_codes[b][:].bitcast(I32))
+        scale_rows = out_2[0].bitcast(I32)
+        for g in range(4):
+            eng = nc.sync if g % 2 == 0 else nc.scalar
+            eng.dma_start(scale_rows[4 * g : 4 * g + 4, :], o_scales[32 * g : 32 * g + 4, :].bitcast(I32))

@@ -41,22 +41,21 @@ def tile_attend_ropeattn_pl_kernel(tc, query, keys, cosn, sinn, size, vals, offs
         sin4 = sinn.rearrange("(p t) c -> p t c", t=PACK)
         vals4 = vals.rearrange("(p t) c -> p t c", t=PACK)
 
+        nc.scalar.dma_start(sz[:], size.rearrange("o (p j) -> p (o j)", j=PACK))
+        nc.sync.dma_start(pos[:], offs2)
+        nc.sync.dma_start(cw[0][:], cos4[:, 0, :])
         nc.sync.dma_start(tok[:], offs)
         nc.sync.dma_start(kw[0][:], keys4[:, 0, :])
-        nc.sync.dma_start(pos[:], offs2)
         nc.sync.dma_start(kw[1][:], keys4[:, 1, :])
-        nc.sync.dma_start(cw[0][:], cos4[:, 0, :])
         nc.sync.dma_start(sw[0][:], sin4[:, 0, :])
         nc.sync.dma_start(vw[0][:], vals4[:, 0, :])
-        nc.sync.dma_start(sz[:], size.rearrange("o (p j) -> p (o j)", j=PACK))
-        nc.sync.dma_start(vw[1][:], vals4[:, 1, :])
+        nc.sync.dma_start(cw[1][:], cos4[:, 2, :])
         nc.sync.dma_start(kw[2][:], keys4[:, 2, :])
         nc.sync.dma_start(kw[3][:], keys4[:, 3, :])
-        nc.sync.dma_start(cw[1][:], cos4[:, 2, :])
         nc.sync.dma_start(sw[1][:], sin4[:, 2, :])
         nc.sync.dma_start(q_raw[:], query.rearrange("(p t) c -> p t c", t=PACK))
-        nc.sync.dma_start(vw[2][:], vals4[:, 2, :])
-        nc.sync.dma_start(vw[3][:], vals4[:, 3, :])
+        for r in range(1, PACK):
+            nc.sync.dma_start(vw[r][:], vals4[:, r, :])
 
         ident = sb.tile([P, P], F32, name="ident")
         make_identity(nc, ident[:])
@@ -77,40 +76,57 @@ def tile_attend_ropeattn_pl_kernel(tc, query, keys, cosn, sinn, size, vals, offs
         pa = sb.tile([P, PACK, I], F32, name="pa")
         pb = sb.tile([P, PACK, I], F32, name="pb")
 
-        vb = [sb.tile([P, T], BF16, name="vb%d" % r) for r in range(PACK)]
-        vg = [sb.tile([P, I], BF16, name="vg%d" % r) for r in range(PACK)]
+        vb = {r: sb.tile([P, T], BF16, name="vb%d" % r) for r in (0, 1, 2)}
+        vg = [sb.tile([P, I], BF16, name="vg%d" % r) for r in range(PACK - 1)]
         vt = sb.tile([P, PACK, P, PACK], BF16, name="vt", align_bytes=64)
         v_codes = sb.tile([P, E], U32, name="v_codes", align_bytes=64)
         v_scales = sb.tile([P, E], U8, name="v_scales", align_bytes=64)
 
-        def rope(j):
-            t0, t1 = 2 * j, 2 * j + 1
-            nc.vector.tensor_copy(kg[t0][:], kw[t0][:].indirect(tok[:]))
-            nc.vector.tensor_copy(kg[t1][:], kw[t1][:].indirect(tok[:]))
-            nc.vector.tensor_copy(cg[j][:], cw[j][:].indirect(pos[:]))
-            nc.vector.tensor_copy(sg[j][:], sw[j][:].indirect(pos[:]))
-            nc.vector.tensor_tensor(pa[:, t0, :], kg[t0][:], cg[j][:], ALU.mult)
-            nc.vector.tensor_tensor(pa[:, t1, :], kg[t1][:], cg[j][:], ALU.mult)
-            nc.vector.tensor_tensor(pb[:, t1, :], kg[t0][:], sg[j][:], ALU.mult)
-            nc.vector.scalar_tensor_tensor(pb[:, t0, :], kg[t1][:], -1.0, sg[j][:], ALU.mult, ALU.mult)
+        v_ps = [ps.tile([P, 2, 2, P], F32, name="v_ps%d" % h) for h in range(2)]
 
-        def values(h):
-            v_ps = ps.tile([P, 2, 2, P], F32, name="v_ps%d" % h)
-            for r in (2 * h, 2 * h + 1):
-                nc.scalar.activation(vb[r][:], vw[r][:], ACT.Copy)
-                nc.scalar.activation(vg[r][:], vb[r][:].indirect(tok[:]), ACT.Copy)
-                words = vg[r][:].bitcast(F32)
-                for u in range(2):
-                    nc.tensor.transpose(v_ps[:, r - 2 * h, u, :], words[:, u::2], ident[:])
-            half = vt[:, 2 * h : 2 * h + 2, :, :].rearrange("p r m t -> p (r m t)")
-            nc.scalar.copy(half.bitcast(F32).rearrange("p (r m u) -> p r m u", r=2, u=2), v_ps[:].rearrange("p r u m -> p r m u"))
-            return half
+        def gather(dst, window, offsets):
+            nc.vector.tensor_copy(dst[:], window[:].indirect(offsets[:]))
+
+        def values_on_scalar(r):
+            nc.scalar.activation(vb[r][:], vw[r][:], ACT.Copy)
+            nc.scalar.activation(vg[r][:], vb[r][:].indirect(tok[:]), ACT.Copy)
+
+        def turn_values(r):
+            words = vg[r][:].bitcast(F32)
+            for u in range(2):
+                nc.tensor.transpose(v_ps[r // 2][:, r % 2, u, :], words[:, u::2], ident[:])
+
+        def lay_values(r0, r1):
+            part = vt[:, r0:r1, :, :].rearrange("p r m t -> p (r m t)")
+            nc.scalar.copy(
+                part.bitcast(F32).rearrange("p (r m u) -> p r m u", r=r1 - r0, u=2),
+                v_ps[r0 // 2][:, r0 % 2 : r0 % 2 + r1 - r0, :, :].rearrange("p r u m -> p r m u"),
+            )
+            return part
 
         def quantize(codes, scales, src):
             nc.vector.quantize_mx(out=codes.bitcast(FP8X4), scales=scales, in_=src)
 
+        nk1 = sb.tile([P, I], F32, name="nk1")
+
+        def rope(j):
+            t0, t1 = 2 * j, 2 * j + 1
+            gather(cg[j], cw[j], pos)
+            for t in (t0, t1):
+                gather(kg[t], kw[t], tok)
+                nc.gpsimd.tensor_tensor(pa[:, t, :], kg[t][:], cg[j][:], ALU.mult)
+            gather(sg[j], sw[j], pos)
+            if j == 0:
+                nc.scalar.activation(nk1[:], kg[t1][:], ACT.Copy, scale=-1.0)
+                nc.gpsimd.tensor_tensor(pb[:, t1, :], kg[t0][:], sg[j][:], ALU.mult)
+                nc.gpsimd.tensor_tensor(pb[:, t0, :], nk1[:], sg[j][:], ALU.mult)
+            else:
+                nc.vector.tensor_tensor(pb[:, t1, :], kg[t0][:], sg[j][:], ALU.mult)
+                nc.vector.scalar_tensor_tensor(pb[:, t0, :], kg[t1][:], -1.0, sg[j][:], ALU.mult, ALU.mult)
+
         rope(0)
-        half0 = values(0)
+        values_on_scalar(0)
+        turn_values(0)
         rope(1)
 
         qb = sb.tile([P, Q, PACK], BF16, name="qb", align_bytes=64)
@@ -118,7 +134,7 @@ def tile_attend_ropeattn_pl_kernel(tc, query, keys, cosn, sinn, size, vals, offs
         q_scales = sb.tile([P, Q], U8, name="q_scales", align_bytes=64)
         nc.scalar.copy(qb[:].rearrange("p (c i) t -> p c t i", i=2), q_raw[:].rearrange("p t (c i) -> p c t i", i=2))
 
-        km = sb.tile([P, I, PACK], BF16, name="km", align_bytes=64)
+        km = sb.tile([P, I, PACK], BF16, name="km", tag="km", align_bytes=64)
         k_codes = sb.tile([P, I], U32, name="k_codes", align_bytes=64)
         k_scales = sb.tile([P, I], U8, name="k_scales", align_bytes=64)
         nc.vector.tensor_tensor(
@@ -129,8 +145,11 @@ def tile_attend_ropeattn_pl_kernel(tc, query, keys, cosn, sinn, size, vals, offs
         )
         quantize(q_codes[:], q_scales[:], qb[:].rearrange("p c t -> p (c t)"))
         quantize(k_codes[:], k_scales[:], km[:].rearrange("p c t -> p (c t)"))
-        quantize(v_codes[:, 0:256], v_scales[:, 0:256], half0)
-        half1 = values(1)
+        for r in (1, 2):
+            values_on_scalar(r)
+            turn_values(r)
+        vg.append(sb.tile([P, I], BF16, name="vg3", tag="km", align_bytes=64))
+        gather(vg[3], vw[3], tok)
 
         stats = [sb.tile([P, 8], F32, name="stats%d" % b) for b in range(2)]
         sums = [sb.tile([P, 8], F32, name="sums%d" % b) for b in range(2)]
@@ -149,7 +168,9 @@ def tile_attend_ropeattn_pl_kernel(tc, query, keys, cosn, sinn, size, vals, offs
         for b in range(2):
             nc.vector.tensor_reduce(stats[b][:, 0:1], sc[b][:], AX.X, ALU.max, negate=True)
             nc.scalar.activation(probs[b][:], sc[b][:], ACT.Exp, bias=stats[b][:, 0:1], accum_out=sums[b][:, 0:1])
-        quantize(v_codes[:, 256:512], v_scales[:, 256:512], half1)
+        half0 = lay_values(0, 2)
+        turn_values(3)
+        half1 = lay_values(2, 4)
         for b in range(2):
             nc.vector.reciprocal(stats[b][:, 1:2], sums[b][:, 0:1])
             nc.vector.scalar_tensor_tensor(
@@ -162,6 +183,8 @@ def tile_attend_ropeattn_pl_kernel(tc, query, keys, cosn, sinn, size, vals, offs
             flat = wt[b][:].rearrange("p q t -> p (q t)")
             nc.scalar.copy(flat.bitcast(F32).rearrange("p (q u) -> p q u", u=2), w_ps[:].rearrange("p u q -> p q u"))
 
+        quantize(v_codes[:, 0:256], v_scales[:, 0:256], half0)
+        quantize(v_codes[:, 256:512], v_scales[:, 256:512], half1)
         o_sb = [sb.tile([P, PACK, P], F32, name="o_sb%d" % b) for b in range(2)]
         ob = [sb.tile([P, P, PACK], BF16, name="ob%d" % b, align_bytes=64) for b in range(2)]
         o_codes = [sb.tile([P, P], U32, name="o_codes%d" % b, align_bytes=64) for b in range(2)]

@@ -41,12 +41,12 @@ def tile_attend_ropeattn_pl_kernel(tc, query, keys, cosn, sinn, size, vals, offs
         sin4 = sinn.rearrange("(p t) c -> p t c", t=PACK)
         vals4 = vals.rearrange("(p t) c -> p t c", t=PACK)
 
-        nc.scalar.dma_start(sz[:], size.rearrange("o (p j) -> p (o j)", j=PACK))
-        nc.sync.dma_start(pos[:], offs2)
         nc.sync.dma_start(cw[0][:], cos4[:, 0, :])
-        nc.sync.dma_start(tok[:], offs)
+        nc.sync.dma_start(pos[:], offs2)
         nc.sync.dma_start(kw[0][:], keys4[:, 0, :])
+        nc.sync.dma_start(tok[:], offs)
         nc.sync.dma_start(kw[1][:], keys4[:, 1, :])
+        nc.sync.dma_start(sz[:], size.rearrange("o (p j) -> p (o j)", j=PACK))
         nc.sync.dma_start(sw[0][:], sin4[:, 0, :])
         nc.sync.dma_start(vw[0][:], vals4[:, 0, :])
         nc.sync.dma_start(cw[1][:], cos4[:, 2, :])
@@ -82,8 +82,6 @@ def tile_attend_ropeattn_pl_kernel(tc, query, keys, cosn, sinn, size, vals, offs
         v_codes = sb.tile([P, E], U32, name="v_codes", align_bytes=64)
         v_scales = sb.tile([P, E], U8, name="v_scales", align_bytes=64)
 
-        v_ps = [ps.tile([P, 2, 2, P], F32, name="v_ps%d" % h) for h in range(2)]
-
         def gather(dst, window, offsets):
             nc.vector.tensor_copy(dst[:], window[:].indirect(offsets[:]))
 
@@ -91,18 +89,17 @@ def tile_attend_ropeattn_pl_kernel(tc, query, keys, cosn, sinn, size, vals, offs
             nc.scalar.activation(vb[r][:], vw[r][:], ACT.Copy)
             nc.scalar.activation(vg[r][:], vb[r][:].indirect(tok[:]), ACT.Copy)
 
-        def turn_values(r):
-            words = vg[r][:].bitcast(F32)
-            for u in range(2):
-                nc.tensor.transpose(v_ps[r // 2][:, r % 2, u, :], words[:, u::2], ident[:])
-
-        def lay_values(r0, r1):
+        def turn_values(r0, r1, bank):
+            v_ps = ps.tile([P, r1 - r0, 2, P], F32, name="v_ps%d" % r0, tag=bank)
+            for r in range(r0, r1):
+                words = vg[r][:].bitcast(F32)
+                for u in range(2):
+                    nc.tensor.transpose(v_ps[:, r - r0, u, :], words[:, u::2], ident[:])
             part = vt[:, r0:r1, :, :].rearrange("p r m t -> p (r m t)")
             nc.scalar.copy(
                 part.bitcast(F32).rearrange("p (r m u) -> p r m u", r=r1 - r0, u=2),
-                v_ps[r0 // 2][:, r0 % 2 : r0 % 2 + r1 - r0, :, :].rearrange("p r u m -> p r m u"),
+                v_ps[:].rearrange("p r u m -> p r m u"),
             )
-            return part
 
         def quantize(codes, scales, src):
             nc.vector.quantize_mx(out=codes.bitcast(FP8X4), scales=scales, in_=src)
@@ -126,7 +123,7 @@ def tile_attend_ropeattn_pl_kernel(tc, query, keys, cosn, sinn, size, vals, offs
 
         rope(0)
         values_on_scalar(0)
-        turn_values(0)
+        turn_values(0, 1, "o_ps0")
         rope(1)
 
         qb = sb.tile([P, Q, PACK], BF16, name="qb", align_bytes=64)
@@ -137,17 +134,19 @@ def tile_attend_ropeattn_pl_kernel(tc, query, keys, cosn, sinn, size, vals, offs
         km = sb.tile([P, I, PACK], BF16, name="km", tag="km", align_bytes=64)
         k_codes = sb.tile([P, I], U32, name="k_codes", align_bytes=64)
         k_scales = sb.tile([P, I], U8, name="k_scales", align_bytes=64)
-        nc.vector.tensor_tensor(
-            km[:].rearrange("p (c i) t -> p c t i", i=2),
-            pa[:].rearrange("p t (c i) -> p c t i", i=2),
-            pb[:].rearrange("p t (c i) -> p c t i", i=2),
-            ALU.add,
-        )
         quantize(q_codes[:], q_scales[:], qb[:].rearrange("p c t -> p (c t)"))
-        quantize(k_codes[:], k_scales[:], km[:].rearrange("p c t -> p (c t)"))
+        halves = [slice(h * I // 2, (h + 1) * I // 2) for h in range(2)]
+        for cols in halves:
+            nc.vector.tensor_tensor(
+                km[:, cols, :].rearrange("p (c i) t -> p c t i", i=2),
+                pa[:, :, cols].rearrange("p t (c i) -> p c t i", i=2),
+                pb[:, :, cols].rearrange("p t (c i) -> p c t i", i=2),
+                ALU.add,
+            )
+        for cols in halves:
+            quantize(k_codes[:, cols], k_scales[:, cols], km[:, cols, :].rearrange("p c t -> p (c t)"))
         for r in (1, 2):
             values_on_scalar(r)
-            turn_values(r)
         vg.append(sb.tile([P, I], BF16, name="vg3", tag="km", align_bytes=64))
         gather(vg[3], vw[3], tok)
 
@@ -158,19 +157,19 @@ def tile_attend_ropeattn_pl_kernel(tc, query, keys, cosn, sinn, size, vals, offs
         wt = [sb.tile([P, P, PACK], BF16, name="wt%d" % b, align_bytes=64) for b in range(2)]
         w_codes = [sb.tile([P, P], U32, name="w_codes%d" % b, align_bytes=64) for b in range(2)]
         w_scales = [sb.tile([P, P], U8, name="w_scales%d" % b, align_bytes=64) for b in range(2)]
-        sc = [ps.tile([P, I], F32, name="sc%d" % b) for b in range(2)]
-        for b in range(2):
-            cols = slice(b * P, (b + 1) * P)
-            nc.tensor.matmul_mx(
-                out=sc[b][:], lhsT=q_codes[:, cols].bitcast(FP8X4), lhsT_scale=q_scales[:, cols],
-                rhs=k_codes[:].bitcast(FP8X4), rhs_scale=k_scales[:], start=True, stop=True,
-            )
+        sc = [ps.tile([P, I], F32, name="sc%d" % b, tag="sc%d" % b) for b in range(2)]
+        for half in halves:
+            for b in range(2):
+                cols = slice(b * P, (b + 1) * P)
+                nc.tensor.matmul_mx(
+                    out=sc[b][:, half], lhsT=q_codes[:, cols].bitcast(FP8X4), lhsT_scale=q_scales[:, cols],
+                    rhs=k_codes[:, half].bitcast(FP8X4), rhs_scale=k_scales[:, half], start=True, stop=True,
+                )
         for b in range(2):
             nc.vector.tensor_reduce(stats[b][:, 0:1], sc[b][:], AX.X, ALU.max, negate=True)
             nc.scalar.activation(probs[b][:], sc[b][:], ACT.Exp, bias=stats[b][:, 0:1], accum_out=sums[b][:, 0:1])
-        half0 = lay_values(0, 2)
-        turn_values(3)
-        half1 = lay_values(2, 4)
+        turn_values(1, 3, "sc0")
+        turn_values(3, 4, "sc1")
         for b in range(2):
             nc.vector.reciprocal(stats[b][:, 1:2], sums[b][:, 0:1])
             nc.vector.scalar_tensor_tensor(
@@ -183,8 +182,9 @@ def tile_attend_ropeattn_pl_kernel(tc, query, keys, cosn, sinn, size, vals, offs
             flat = wt[b][:].rearrange("p q t -> p (q t)")
             nc.scalar.copy(flat.bitcast(F32).rearrange("p (q u) -> p q u", u=2), w_ps[:].rearrange("p u q -> p q u"))
 
-        quantize(v_codes[:, 0:256], v_scales[:, 0:256], half0)
-        quantize(v_codes[:, 256:512], v_scales[:, 256:512], half1)
+        for h in range(2):
+            cols = slice(2 * h * P, 2 * (h + 1) * P)
+            quantize(v_codes[:, cols], v_scales[:, cols], vt[:, 2 * h : 2 * h + 2, :, :].rearrange("p r m t -> p (r m t)"))
         o_sb = [sb.tile([P, PACK, P], F32, name="o_sb%d" % b) for b in range(2)]
         ob = [sb.tile([P, P, PACK], BF16, name="ob%d" % b, align_bytes=64) for b in range(2)]
         o_codes = [sb.tile([P, P], U32, name="o_codes%d" % b, align_bytes=64) for b in range(2)]
@@ -194,14 +194,15 @@ def tile_attend_ropeattn_pl_kernel(tc, query, keys, cosn, sinn, size, vals, offs
         for b in range(2):
             cols = slice(b * P, (b + 1) * P)
             quantize(w_codes[b][:], w_scales[b][:], wt[b][:].rearrange("p q t -> p (q t)"))
-            o_ps = ps.tile([P, PACK, P], F32, name="o_ps%d" % b)
-            for r in range(PACK):
-                rows = slice(r * P, (r + 1) * P)
-                nc.tensor.matmul_mx(
-                    out=o_ps[:, r, :], lhsT=v_codes[:, rows].bitcast(FP8X4), lhsT_scale=v_scales[:, rows],
-                    rhs=w_codes[b][:].bitcast(FP8X4), rhs_scale=w_scales[b][:], start=True, stop=True,
-                )
-            nc.scalar.copy(o_sb[b][:], o_ps[:])
+            for h in range(2):
+                o_ps = ps.tile([P, 2, P], F32, name="o_ps", tag="o_ps%d" % (2 * b + h))
+                for r in (2 * h, 2 * h + 1):
+                    rows = slice(r * P, (r + 1) * P)
+                    nc.tensor.matmul_mx(
+                        out=o_ps[:, r % 2, :], lhsT=v_codes[:, rows].bitcast(FP8X4), lhsT_scale=v_scales[:, rows],
+                        rhs=w_codes[b][:].bitcast(FP8X4), rhs_scale=w_scales[b][:], start=True, stop=True,
+                    )
+                nc.scalar.copy(o_sb[b][:, 2 * h : 2 * h + 2, :], o_ps[:])
             nc.scalar.dma_start(out4[:, :, cols], o_sb[b][:])
         for b in range(2):
             cols = slice(b * P, (b + 1) * P)

from contextlib import ExitStack

import concourse.mybir as mybir
from concourse.masks import make_identity

D, T, I, Q, E = 512, 1024, 512, 256, 512
FLOPS = 2 * Q * I * D + 2 * E * Q * I
BYTES = 4 * (D * Q + D * T + D * T + I + E * T + E * Q) + 2 * 2 * 128 * 32 + E * Q + 16 * Q

F32 = mybir.dt.float32
BF16 = mybir.dt.bfloat16
I32 = mybir.dt.int32
U32 = mybir.dt.uint32
U16 = mybir.dt.uint16
U8 = mybir.dt.uint8
FP8X4 = mybir.dt.float8_e4m3fn_x4
ALU = mybir.AluOpType
ACT = mybir.ActivationFunctionType
AX = mybir.AxisListType

P = 128
PACK = 4


def tile_attend_ropeattn_pl_kernel(tc, query, keys, cosn, sinn, size, vals, offs, offs2, out_0, out_1, out_2):
    nc = tc.nc
    with ExitStack() as ctx:
        sb = ctx.enter_context(tc.tile_pool(name="sb", bufs=1))
        ps = ctx.enter_context(tc.psum_pool(name="ps", bufs=1))

        tok = sb.tile([P, I // 16], U16, name="tok")
        pos = sb.tile([P, I // 16], U16, name="pos")
        kw = [sb.tile([P, T], F32, name="kw%d" % t) for t in range(PACK)]
        cw = [sb.tile([P, T], F32, name="cw%d" % j) for j in range(2)]
        sw = [sb.tile([P, T], F32, name="sw%d" % j) for j in range(2)]
        vw = [sb.tile([P, T], F32, name="vw%d" % t) for t in range(PACK)]
        q_raw = sb.tile([P, PACK, Q], F32, name="q_raw")
        sz = sb.tile([P, PACK], F32, name="sz")
        keys4 = keys.rearrange("(p t) c -> p t c", t=PACK)
        cos4 = cosn.rearrange("(p t) c -> p t c", t=PACK)
        sin4 = sinn.rearrange("(p t) c -> p t c", t=PACK)
        vals4 = vals.rearrange("(p t) c -> p t c", t=PACK)

        nc.sync.dma_start(cw[0][:], cos4[:, 0, :])
        nc.sync.dma_start(pos[:], offs2)
        nc.sync.dma_start(kw[0][:], keys4[:, 0, :])
        nc.sync.dma_start(tok[:], offs)
        nc.sync.dma_start(kw[1][:], keys4[:, 1, :])
        nc.sync.dma_start(sz[:], size.rearrange("o (p j) -> p (o j)", j=PACK))
        nc.sync.dma_start(sw[0][:], sin4[:, 0, :])
        nc.sync.dma_start(vw[0][:], vals4[:, 0, :])
        nc.sync.dma_start(cw[1][:], cos4[:, 2, :])
        nc.sync.dma_start(kw[2][:], keys4[:, 2, :])
        nc.sync.dma_start(kw[3][:], keys4[:, 3, :])
        nc.sync.dma_start(sw[1][:], sin4[:, 2, :])
        nc.sync.dma_start(q_raw[:], query.rearrange("(p t) c -> p t c", t=PACK))
        for r in range(1, PACK):
            nc.sync.dma_start(vw[r][:], vals4[:, r, :])

        ident = sb.tile([P, P], F32, name="ident")
        make_identity(nc, ident[:])

        warm = sb.tile([P, 8], F32, name="warm")
        nc.vector.memset(warm[:, 0:1], 0.0)
        nc.scalar.activation(warm[:, 4:5], warm[:, 0:1], ACT.Exp)

        sz_ps = ps.tile([P, PACK, P], F32, name="sz_ps", tag="w_ps0")
        for j in range(PACK):
            nc.tensor.transpose(sz_ps[:, j, :], sz[:, j : j + 1].to_broadcast([P, P]), ident[:])
        szb = sb.tile([P, P, PACK], F32, name="szb")
        nc.scalar.copy(szb[:], sz_ps[:].rearrange("p j n -> p n j"))

        kg = [sb.tile([P, I], F32, name="kg%d" % t) for t in range(PACK)]
        cg = [sb.tile([P, I], F32, name="cg%d" % j) for j in range(2)]
        sg = [sb.tile([P, I], F32, name="sg%d" % j) for j in range(2)]
        pa = sb.tile([P, PACK, I], F32, name="pa")
        pb = sb.tile([P, PACK, I], F32, name="pb")

        vb = {r: sb.tile([P, T], BF16, name="vb%d" % r) for r in (0, 1, 2)}
        vg = [sb.tile([P, I], BF16, name="vg%d" % r) for r in range(PACK - 1)]
        vt = sb.tile([P, PACK, P, PACK], BF16, name="vt", align_bytes=64)
        v_codes = sb.tile([P, E], U32, name="v_codes", align_bytes=64)
        v_scales = sb.tile([P, E], U8, name="v_scales", align_bytes=64)

        def gather(dst, window, offsets):
            nc.vector.tensor_copy(dst[:], window[:].indirect(offsets[:]))

        def values_on_scalar(r):
            nc.scalar.activation(vb[r][:], vw[r][:], ACT.Copy)
            nc.scalar.activation(vg[r][:], vb[r][:].indirect(tok[:]), ACT.Copy)

        def turn_values(r0, r1, bank):
            v_ps = ps.tile([P, r1 - r0, 2, P], F32, name="v_ps%d" % r0, tag=bank)
            for r in range(r0, r1):
                words = vg[r][:].bitcast(F32)
                for u in range(2):
                    nc.tensor.transpose(v_ps[:, r - r0, u, :], words[:, u::2], ident[:])
            part = vt[:, r0:r1, :, :].rearrange("p r m t -> p (r m t)")
            nc.scalar.copy(
                part.bitcast(F32).rearrange("p (r m u) -> p r m u", r=r1 - r0, u=2),
                v_ps[:].rearrange("p r u m -> p r m u"),
            )

        def quantize(codes, scales, src):
            nc.vector.quantize_mx(out=codes.bitcast(FP8X4), scales=scales, in_=src)

        nk1 = sb.tile([P, I], F32, name="nk1")

        def rope(j):
            t0, t1 = 2 * j, 2 * j + 1
            gather(cg[j], cw[j], pos)
            for t in (t0, t1):
                gather(kg[t], kw[t], tok)
                nc.gpsimd.tensor_tensor(pa[:, t, :], kg[t][:], cg[j][:], ALU.mult)
            gather(sg[j], sw[j], pos)
            if j == 0:
                nc.scalar.activation(nk1[:], kg[t1][:], ACT.Copy, scale=-1.0)
                nc.gpsimd.tensor_tensor(pb[:, t1, :], kg[t0][:], sg[j][:], ALU.mult)
                nc.gpsimd.tensor_tensor(pb[:, t0, :], nk1[:], sg[j][:], ALU.mult)
            else:
                nc.vector.tensor_tensor(pb[:, t1, :], kg[t0][:], sg[j][:], ALU.mult)
                nc.vector.scalar_tensor_tensor(pb[:, t0, :], kg[t1][:], -1.0, sg[j][:], ALU.mult, ALU.mult)

        rope(0)
        values_on_scalar(0)
        turn_values(0, 1, "o_ps0")
        rope(1)

        qb = sb.tile([P, Q, PACK], BF16, name="qb", align_bytes=64)
        q_codes = sb.tile([P, Q], U32, name="q_codes", align_bytes=64)
        q_scales = sb.tile([P, Q], U8, name="q_scales", align_bytes=64)
        nc.scalar.copy(qb[:].rearrange("p (c i) t -> p c t i", i=2), q_raw[:].rearrange("p t (c i) -> p c t i", i=2))

        km = sb.tile([P, I, PACK], BF16, name="km", tag="km", align_bytes=64)
        k_codes = sb.tile([P, I], U32, name="k_codes", align_bytes=64)
        k_scales = sb.tile([P, I], U8, name="k_scales", align_bytes=64)
        quantize(q_codes[:], q_scales[:], qb[:].rearrange("p c t -> p (c t)"))
        halves = [slice(h * I // 2, (h + 1) * I // 2) for h in range(2)]
        for cols in halves:
            nc.vector.tensor_tensor(
                km[:, cols, :].rearrange("p (c i) t -> p c t i", i=2),
                pa[:, :, cols].rearrange("p t (c i) -> p c t i", i=2),
                pb[:, :, cols].rearrange("p t (c i) -> p c t i", i=2),
                ALU.add,
            )
        for cols in halves:
            quantize(k_codes[:, cols], k_scales[:, cols], km[:, cols, :].rearrange("p c t -> p (c t)"))
        for r in (1, 2):
            values_on_scalar(r)
        vg.append(sb.tile([P, I], BF16, name="vg3", tag="km", align_bytes=64))
        gather(vg[3], vw[3], tok)

        stats = [sb.tile([P, 8], F32, name="stats%d" % b) for b in range(2)]
        sums = [sb.tile([P, 8], F32, name="sums%d" % b) for b in range(2)]
        probs = [sb.tile([P, I], F32, name="probs%d" % b) for b in range(2)]
        wb = [sb.tile([P, I], BF16, name="wb%d" % b) for b in range(2)]
        wt = [sb.tile([P, P, PACK], BF16, name="wt%d" % b, align_bytes=64) for b in range(2)]
        w_codes = [sb.tile([P, P], U32, name="w_codes%d" % b, align_bytes=64) for b in range(2)]
        w_scales = [sb.tile([P, P], U8, name="w_scales%d" % b, align_bytes=64) for b in range(2)]
        sc = [ps.tile([P, I], F32, name="sc%d" % b, tag="sc%d" % b) for b in range(2)]
        for half in halves:
            for b in range(2):
                cols = slice(b * P, (b + 1) * P)
                nc.tensor.matmul_mx(
                    out=sc[b][:, half], lhsT=q_codes[:, cols].bitcast(FP8X4), lhsT_scale=q_scales[:, cols],
                    rhs=k_codes[:, half].bitcast(FP8X4), rhs_scale=k_scales[:, half], start=True, stop=True,
                )
        for b in range(2):
            nc.vector.tensor_reduce(stats[b][:, 0:1], sc[b][:], AX.X, ALU.max, negate=True)
            nc.scalar.activation(probs[b][:], sc[b][:], ACT.Exp, bias=stats[b][:, 0:1], accum_out=sums[b][:, 0:1])
        turn_values(1, 3, "sc0")
        turn_values(3, 4, "sc1")
        for b in range(2):
            nc.vector.reciprocal(stats[b][:, 1:2], sums[b][:, 0:1])
            nc.vector.scalar_tensor_tensor(
                wb[b][:], probs[b][:], stats[b][:, 1:2], szb[:].rearrange("p n j -> p (n j)"), ALU.mult, ALU.mult
            )
            w_ps = ps.tile([P, 2, P], F32, name="w_ps", tag="w_ps%d" % b)
            words = wb[b][:].bitcast(F32)
            for u in range(2):
                nc.tensor.transpose(w_ps[:, u, :], words[:, u::2], ident[:])
            flat = wt[b][:].rearrange("p q t -> p (q t)")
            nc.scalar.copy(flat.bitcast(F32).rearrange("p (q u) -> p q u", u=2), w_ps[:].rearrange("p u q -> p q u"))

        for h in range(2):
            cols = slice(2 * h * P, 2 * (h + 1) * P)
            quantize(v_codes[:, cols], v_scales[:, cols], vt[:, 2 * h : 2 * h + 2, :, :].rearrange("p r m t -> p (r m t)"))
        o_sb = [sb.tile([P, PACK, P], F32, name="o_sb%d" % b) for b in range(2)]
        ob = [sb.tile([P, P, PACK], BF16, name="ob%d" % b, align_bytes=64) for b in range(2)]
        o_codes = [sb.tile([P, P], U32, name="o_codes%d" % b, align_bytes=64) for b in range(2)]
        o_scales = sb.tile([P, Q], U8, name="o_scales", align_bytes=64)
        out4 = out_0.rearrange("(p r) q -> p r q", r=PACK)
        words_out = out_1[0].rearrange("l c r -> l (c r)").bitcast(I32)
        for b in range(2):
            cols = slice(b * P, (b + 1) * P)
            quantize(w_codes[b][:], w_scales[b][:], wt[b][:].rearrange("p q t -> p (q t)"))
            for h in range(2):
                o_ps = ps.tile([P, 2, P], F32, name="o_ps", tag="o_ps%d" % (2 * b + h))
                for r in (2 * h, 2 * h + 1):
                    rows = slice(r * P, (r + 1) * P)
                    nc.tensor.matmul_mx(
                        out=o_ps[:, r % 2, :], lhsT=v_codes[:, rows].bitcast(FP8X4), lhsT_scale=v_scales[:, rows],
                        rhs=w_codes[b][:].bitcast(FP8X4), rhs_scale=w_scales[b][:], start=True, stop=True,
                    )
                nc.scalar.copy(o_sb[b][:, 2 * h : 2 * h + 2, :], o_ps[:])
            nc.scalar.dma_start(out4[:, :, cols], o_sb[b][:])
        for b in range(2):
            cols = slice(b * P, (b + 1) * P)
            nc.vector.tensor_copy(
                ob[b][:].rearrange("p (c i) r -> p c r i", i=2), o_sb[b][:].rearrange("p r (c i) -> p c r i", i=2)
            )
            quantize(o_codes[b][:], o_scales[:, cols], ob[b][:].rearrange("p q r -> p (q r)"))
            nc.sync.dma_start(words_out[:, cols], o_codes[b][:].bitcast(I32))
        scale_rows = out_2[0].bitcast(I32)
        for g in range(4):
            eng = nc.sync if g % 2 == 0 else nc.scalar
            eng.dma_start(scale_rows[4 * g : 4 * g + 4, :], o_scales[32 * g : 32 * g + 4, :].bitcast(I32))
